import numpy as np
import ml_dtypes


def mxq(x, axis, fmt="e4m3"):
    dtype, down = {"e4m3": (ml_dtypes.float8_e4m3fn, 7), "e5m2": (ml_dtypes.float8_e5m2, 14)}[fmt]
    v = np.moveaxis(np.asarray(x, np.float32).astype(ml_dtypes.bfloat16).astype(np.float64), axis, -1)
    blocks = v.reshape(v.shape[:-1] + (-1, 32))
    amax = np.abs(blocks).max(-1, keepdims=True)
    byte = np.maximum(np.where(amax > 0, np.frexp(amax)[1] - 1 + 127, 0) - down, 1)
    scale = np.exp2(byte - 127.0)
    codes = (blocks / scale).astype(np.float32).astype(dtype).astype(np.float64)
    return np.moveaxis((codes * scale).reshape(v.shape), -1, axis)


WIDE = False


def mx_kscale(k):
    if not WIDE:
        return np.ones(k)
    levels = np.array([10, -10, 5, -5, 0])
    if k % 512:
        return np.exp2(np.random.permutation(np.resize(levels, k // 32))).repeat(32)
    a = np.empty((k // 512, 16))
    for p in range(k // 512):
        a[p, :8] = np.random.permutation(np.resize(levels, 8))
        for g in range(8):
            far = levels[np.abs(levels - a[p, g]) >= 10]
            a[p, g + 8] = far[np.random.randint(len(far))]
    return np.exp2(a.ravel()).repeat(32)


def f64(x):
    return np.asarray(x).astype(np.float64)


def striped(idx):
    return np.tile(idx.reshape(-1, 16).T, (8, 1)).astype(np.uint16)


def unstriped(offs):
    return offs[:16].T.reshape(-1).astype(np.int64)


E2M1 = np.array([0.0, 0.5, 1.0, 1.5, 2.0, 3.0, 4.0, 6.0, -0.0, -0.5, -1.0, -1.5, -2.0, -3.0, -4.0, -6.0])


def pack_weight(w, fmt):
    k, n = w.shape
    w = f64(np.asarray(w, np.float32).astype(ml_dtypes.bfloat16)).reshape(k // 32, 32, n)
    amax = np.abs(w).max(1)
    if fmt == "e4m3":
        byte = np.frexp(amax)[1] - 1 + 127 - 7
    else:
        mant, ex = np.frexp(amax / 6.0)
        byte = np.where(mant > 0.5, ex, ex - 1) + 127
    byte = np.clip(np.where(amax > 0, byte, 1), 1, 254)
    scaled = (w * np.exp2(127.0 - byte)[:, None, :]).reshape(k, n).astype(np.float32)
    by_word = np.ascontiguousarray(scaled.reshape(k // 512, 128, 4, n).transpose(0, 1, 3, 2))
    if fmt == "e4m3":
        words = by_word.astype(ml_dtypes.float8_e4m3fn).view(np.uint8)
    else:
        c = by_word.astype(ml_dtypes.float4_e2m1fn).view(np.uint8) & 0xF
        words = (c[..., 0::2] | (c[..., 1::2] << 4)).reshape(k // 512, 128, 2 * n)
    return np.ascontiguousarray(words), np.ascontiguousarray(byte.astype(np.uint8).reshape(k // 512, 16, n))


def unpack_weight(words, scales, fmt):
    g, _, n = scales.shape
    words = np.ascontiguousarray(words).reshape(g, 128, n, -1)
    if fmt == "e4m3":
        vals = words.view(ml_dtypes.float8_e4m3fn).astype(np.float64)
    else:
        nib = np.empty((g, 128, n, 4), np.uint8)
        nib[..., 0::2] = words & 0xF
        nib[..., 1::2] = words >> 4
        vals = E2M1[nib]
    vals = vals * np.repeat(np.exp2(scales.astype(np.float64) - 127.0), 8, axis=1)[..., None]
    return vals.transpose(0, 1, 3, 2).reshape(g * 512, n)


def gelu(v):
    return 0.5 * v * (1.0 + np.tanh(np.sqrt(2.0 / np.pi) * (v + 0.044715 * v**3)))


K, H, N, T, S, P, P2 = 1024, 512, 512, 4096, 2048, 1024, 512

def setup_inputs():
    n = np.random.standard_normal
    s = mx_kscale(K)[:, None]
    u = mx_kscale(H)[:, None]
    tab_words, tab_scales = pack_weight(n((K, T)) * s, "e4m3")
    w4_words, w4_scales = pack_weight(1.3 * n((K, H)) / np.sqrt(K) / s, "e2m1")
    gain = (np.exp(0.3 * n(H)) * np.sqrt(u[:, 0])).astype(np.float32)
    w2 = (n((H, N)) / np.sqrt(H) / u).astype(np.float32)
    b2 = (0.5 * n(N)).astype(np.float32)
    return {"tab_words": tab_words, "tab_scales": tab_scales,
            "w4_words": w4_words, "w4_scales": w4_scales,
            "gain": gain, "w2": w2, "b2": b2,
            "offs": striped(np.random.permutation(T)[:S]),
            "pos1": striped(np.random.permutation(S)[:P]),
            "pos2": striped(np.random.permutation(S)[:P]),
            "pos3": striped(np.random.permutation(P)[:P2]),
            "pos4": striped(np.random.permutation(S)[:P2])}

def reference(tab_words, tab_scales, w4_words, w4_scales, gain, w2, b2, offs, pos1, pos2, pos3, pos4):
    v = unpack_weight(tab_words, tab_scales, "e4m3")[:, unstriped(offs)]
    w4 = unpack_weight(w4_words, w4_scales, "e2m1")
    h = f64(gain)[:, None] * np.tanh(w4.T @ v)
    a1 = h[:, unstriped(pos1)] + h[:, unstriped(pos2)]
    paper = h[:, unstriped(pos4)]
    a2 = (a1[:, unstriped(pos3)] - paper) * paper
    w2q = mxq(f64(w2), 0, "e4m3")
    a2q = mxq(a2, 0, "e4m3")
    y = (w2q.T @ a2q) + f64(b2)[:, None]
    return np.tanh(y)

@@ -1,0 +1,202 @@
+from contextlib import ExitStack
+
+import concourse.mybir as mybir
+
+K, H, N, T, S, PAIRS, KEPT = 1024, 512, 512, 4096, 2048, 1024, 512
+FLOPS = 2 * K * H * S + 2 * H * N * KEPT
+
+F32 = mybir.dt.float32
+BF16 = mybir.dt.bfloat16
+I32 = mybir.dt.int32
+U32 = mybir.dt.uint32
+U16 = mybir.dt.uint16
+U8 = mybir.dt.uint8
+FP8X4 = mybir.dt.float8_e4m3fn_x4
+FP4X4 = mybir.dt.float4_e2m1fn_x4
+ACT = mybir.ActivationFunctionType
+ALU = mybir.AluOpType
+
+P = 128
+PASSES = 2
+SLOTS = 4
+BANK = 512
+PER_COL = 16
+FIRST_CHUNKS = [(0, 512), (512, 1024), (1024, 1536), (1536, 1792), (1792, 2048)]
+BANK_CHUNKS = [(c, c + BANK) for c in range(0, S, BANK)]
+FIRST_GAIN_SPLIT = 1024
+TAIL_CHUNKS = [(0, 256), (256, 384), (384, 512)]
+
+
+def entries(lst, lo, hi):
+    return lst[:, lo // PER_COL : hi // PER_COL]
+
+
+def tile_list_manifest_paper_scores_kernel(
+    tc, tab_words, tab_scales, w4_words, w4_scales, gain, w2, b2, offs, pos1, pos2, pos3, pos4, out
+):
+    nc = tc.nc
+    with ExitStack() as ctx:
+        lists = ctx.enter_context(tc.tile_pool(name="lists", bufs=1))
+        keep = ctx.enter_context(tc.tile_pool(name="keep", bufs=1))
+        ring = ctx.enter_context(tc.tile_pool(name="ring", bufs=2))
+        psum = ctx.enter_context(tc.psum_pool(name="psum", bufs=8))
+
+        idx = lists.tile([P, S // PER_COL], U16, name="idx")
+        p1 = lists.tile([P, PAIRS // PER_COL], U16, name="p1")
+        p2 = lists.tile([P, PAIRS // PER_COL], U16, name="p2")
+        p3 = lists.tile([P, KEPT // PER_COL], U16, name="p3")
+        p4 = lists.tile([P, KEPT // PER_COL], U16, name="p4")
+        nc.sync.dma_start(idx[:], offs)
+
+        tab_bytes = keep.tile([P, T], U8, name="tab_bytes", align_bytes=64)
+        nc.sync.dma_start(
+            tab_bytes[0:32, :].bitcast(I32),
+            tab_scales.rearrange("a q t -> q a t").bitcast(I32),
+        )
+        nc.vector.memset(tab_bytes[32:64, :].bitcast(I32), 0)
+        nc.vector.memset(tab_bytes[64:128, :].bitcast(I32), 0)
+
+        table = [
+            keep.tile([P, T], I32, name="table%d" % a, tag="table%d" % a, align_bytes=64)
+            for a in range(PASSES)
+        ]
+        words = [tab_words[a].rearrange("p n i -> p (n i)").bitcast(I32) for a in range(PASSES)]
+        nc.sync.dma_start(table[0][:], words[0])
+
+        w4_raw = keep.tile([P, PASSES, H // 2], I32, name="w4_raw", align_bytes=64)
+        nc.sync.dma_start(w4_raw[:], w4_words.rearrange("a p b -> p a b").bitcast(I32))
+        for tile, src in ((p1, pos1), (p4, pos4), (p2, pos2), (p3, pos3)):
+            nc.sync.dma_start(tile[:], src)
+        nc.sync.dma_start(table[1][:], words[1])
+
+        w4s_raw = keep.tile([P, PASSES, H // 4], I32, name="w4s_raw", align_bytes=64)
+        w4s_rows = w4_scales.rearrange("a q c -> q a c").bitcast(I32)
+        for quad in range(4):
+            nc.gpsimd.dma_start(w4s_raw[32 * quad : 32 * quad + 4], w4s_rows[4 * quad : 4 * quad + 4])
+        gains = [keep.tile([P, 1], F32, name="gain%d" % t) for t in range(SLOTS)]
+        gain_rows = gain.rearrange("(g t j) -> t g j", t=SLOTS, j=8)
+        with nc.allow_non_contiguous_dma(reason="one gain value to a partition"):
+            for t in range(SLOTS):
+                nc.gpsimd.dma_start(gains[t][:], gain_rows[t])
+        bias = keep.tile([P, SLOTS], F32, name="bias")
+        nc.gpsimd.dma_start(bias[:], b2.rearrange("(p j) -> p j", j=SLOTS))
+
+        w4_codes = keep.tile([P, PASSES, SLOTS, 2 * P], U8, name="w4_codes", align_bytes=64)
+        w4_plane = keep.tile([P, PASSES, SLOTS, P], U8, name="w4_plane", align_bytes=64)
+        nc.vector.memset(w4_plane[:].bitcast(I32), 0)
+        nc.scalar.copy(
+            w4_codes[:].bitcast(U32).rearrange("p a t (g w) -> p a t g w", w=4),
+            w4_raw[:].bitcast(U32).rearrange("p a (g t w) -> p a t g w", t=SLOTS, w=4),
+        )
+        for quad in range(4):
+            rows = slice(32 * quad, 32 * quad + 4)
+            nc.scalar.copy(
+                w4_plane[rows].bitcast(U32).rearrange("p a t (g w) -> p a t g w", w=2),
+                w4s_raw[rows].bitcast(U32).rearrange("p a (g t w) -> p a t g w", t=SLOTS, w=2),
+            )
+
+        v_plane = keep.tile([P, PASSES, S], U8, name="v_plane", align_bytes=64)
+        nc.vector.memset(v_plane[:].bitcast(I32), 0)
+        picked_bytes = keep.tile([P, S], U8, name="picked_bytes", align_bytes=64)
+        nc.vector.tensor_copy(picked_bytes[:], tab_bytes[:].indirect(idx[:]))
+        for quad in range(4):
+            nc.scalar.dma_start(
+                v_plane[32 * quad : 32 * quad + 4].bitcast(I32),
+                picked_bytes[8 * quad : 8 * quad + 8, :].bitcast(I32),
+            )
+
+        v_codes = [keep.tile([P, S], U32, name="v_codes%d" % a, align_bytes=64) for a in range(PASSES)]
+        nc.vector.tensor_copy(v_codes[0][:], table[0][:].bitcast(U32).indirect(idx[:]))
+        for lo, hi in FIRST_CHUNKS:
+            nc.vector.tensor_copy(v_codes[1][:, lo:hi], table[1][:].bitcast(U32).indirect(entries(idx, lo, hi)))
+
+        w2_raw = keep.tile([P, SLOTS, N], F32, name="w2_raw", tag="table0", align_bytes=64)
+        w2_rows = w2.rearrange("(g t j) n -> t g j n", t=SLOTS, j=8)
+        for t in range(SLOTS):
+            nc.sync.dma_start(w2_raw[:, t, :], w2_rows[t])
+
+        h = [keep.tile([P, S], F32, name="h%d" % t) for t in range(SLOTS)]
+
+        def first_stage(t):
+            squashed = ring.tile([P, S], F32, name="squashed")
+            for lo, hi in FIRST_CHUNKS if t == 0 else BANK_CHUNKS:
+                acc = psum.tile([P, BANK], F32, name="acc")
+                for a in range(PASSES):
+                    nc.tensor.matmul_mx(
+                        out=acc[:, : hi - lo],
+                        lhsT=w4_codes[:, a, t, :].bitcast(FP4X4),
+                        lhsT_scale=w4_plane[:, a, t, :],
+                        rhs=v_codes[a][:, lo:hi].bitcast(FP8X4),
+                        rhs_scale=v_plane[:, a, lo:hi],
+                        start=(a == 0),
+                        stop=(a == PASSES - 1),
+                    )
+                nc.scalar.activation(squashed[:, lo:hi], acc[:, : hi - lo], ACT.Tanh)
+                if t > 0 or hi <= FIRST_GAIN_SPLIT:
+                    nc.scalar.activation(h[t][:, lo:hi], squashed[:, lo:hi], ACT.Copy, scale=gains[t][:])
+                else:
+                    nc.vector.tensor_scalar(h[t][:, lo:hi], squashed[:, lo:hi], gains[t][:], None, ALU.mult)
+
+        paper = keep.tile([P, SLOTS, KEPT], F32, name="paper")
+        diff = keep.tile([P, SLOTS, KEPT], F32, name="diff")
+        a1 = [keep.tile([P, PAIRS], F32, name="a1_%d" % t) for t in range(SLOTS)]
+
+        def kept_minus_paper(t, lo, hi):
+            nc.vector.tensor_tensor(
+                diff[:, t, lo:hi], a1[t][:].indirect(entries(p3, lo, hi)), paper[:, t, lo:hi], ALU.subtract
+            )
+
+        for t in range(SLOTS):
+            first_stage(t)
+            left = ring.tile([P, PAIRS], F32, name="left")
+            nc.vector.tensor_copy(left[:], h[t][:].indirect(p1[:]))
+            if t > 0:
+                kept_minus_paper(t - 1, 0, KEPT)
+            nc.vector.tensor_copy(paper[:, t, :], h[t][:].indirect(p4[:]))
+            nc.vector.tensor_tensor(a1[t][:], h[t][:].indirect(p2[:]), left[:], ALU.add)
+
+        w2_grouped = keep.tile([P, SLOTS, P, SLOTS], BF16, name="w2_grouped", align_bytes=64)
+        nc.scalar.copy(
+            w2_grouped[:].rearrange("p j m t -> p m t j"),
+            w2_raw[:].rearrange("p t (m j) -> p m t j", j=SLOTS),
+        )
+        w2_codes = keep.tile([P, N], U32, name="w2_codes", align_bytes=64)
+        w2_plane = keep.tile([P, N], U8, name="w2_plane", align_bytes=64)
+        nc.vector.quantize_mx(
+            out=w2_codes[:].bitcast(FP8X4),
+            scales=w2_plane[:],
+            in_=w2_grouped[:].rearrange("p j m t -> p (j m t)"),
+        )
+
+        out_rows = out.rearrange("(p j) m -> p j m", j=SLOTS)
+        for c, (lo, hi) in enumerate(TAIL_CHUNKS):
+            width = hi - lo
+            kept_minus_paper(SLOTS - 1, lo, hi)
+            a2 = keep.tile([P, width, SLOTS], BF16, name="a2_%d" % c, align_bytes=64)
+            nc.vector.tensor_tensor(
+                a2[:].rearrange("p (c i) t -> p c t i", i=4),
+                diff[:, :, lo:hi].rearrange("p t (c i) -> p c t i", i=4),
+                paper[:, :, lo:hi].rearrange("p t (c i) -> p c t i", i=4),
+                ALU.mult,
+            )
+            a2_codes = keep.tile([P, width], U32, name="a2_codes%d" % c, align_bytes=64)
+            a2_plane = keep.tile([P, width], U8, name="a2_plane%d" % c, align_bytes=64)
+            nc.vector.quantize_mx(
+                out=a2_codes[:].bitcast(FP8X4),
+                scales=a2_plane[:],
+                in_=a2[:].rearrange("p m t -> p (m t)"),
+            )
+            scores = keep.tile([P, SLOTS, width], F32, name="scores%d" % c)
+            for j in range(SLOTS):
+                acc = psum.tile([P, BANK], F32, name="acc")
+                nc.tensor.matmul_mx(
+                    out=acc[:, :width],
+                    lhsT=w2_codes[:, j * P : (j + 1) * P].bitcast(FP8X4),
+                    lhsT_scale=w2_plane[:, j * P : (j + 1) * P],
+                    rhs=a2_codes[:].bitcast(FP8X4),
+                    rhs_scale=a2_plane[:],
+                    start=True,
+                    stop=True,
+                )
+                nc.scalar.activation(scores[:, j, :], acc[:, :width], ACT.Tanh, bias=bias[:, j : j + 1])
+            nc.sync.dma_start(out_rows[:, :, lo:hi], scores[:])

@@ -56,6 +56,15 @@ def tile_list_manifest_paper_scores_kernel(
         nc.vector.memset(tab_bytes[32:64, :].bitcast(I32), 0)
         nc.vector.memset(tab_bytes[64:128, :].bitcast(I32), 0)
 
+        w4s_raw = keep.tile([P, PASSES, H // 4], I32, name="w4s_raw", align_bytes=64)
+        w4s_rows = w4_scales.rearrange("a q c -> q a c").bitcast(I32)
+        for quad in range(4):
+            nc.scalar.dma_start(w4s_raw[32 * quad : 32 * quad + 4], w4s_rows[4 * quad : 4 * quad + 4])
+        gain_rows = gain.rearrange("(g t j) -> t g j", t=SLOTS, j=8)
+        gain0 = keep.tile([P, 1], F32, name="gain0")
+        with nc.allow_non_contiguous_dma(reason="one gain value to a partition"):
+            nc.scalar.dma_start(gain0[:], gain_rows[0])
+
         table = [
             keep.tile([P, T], I32, name="table%d" % a, tag="table%d" % a, align_bytes=64)
             for a in range(PASSES)
@@ -68,18 +77,6 @@ def tile_list_manifest_paper_scores_kernel(
         for tile, src in ((p1, pos1), (p4, pos4), (p2, pos2), (p3, pos3)):
             nc.sync.dma_start(tile[:], src)
         nc.sync.dma_start(table[1][:], words[1])
-
-        w4s_raw = keep.tile([P, PASSES, H // 4], I32, name="w4s_raw", align_bytes=64)
-        w4s_rows = w4_scales.rearrange("a q c -> q a c").bitcast(I32)
-        for quad in range(4):
-            nc.gpsimd.dma_start(w4s_raw[32 * quad : 32 * quad + 4], w4s_rows[4 * quad : 4 * quad + 4])
-        gains = [keep.tile([P, 1], F32, name="gain%d" % t) for t in range(SLOTS)]
-        gain_rows = gain.rearrange("(g t j) -> t g j", t=SLOTS, j=8)
-        with nc.allow_non_contiguous_dma(reason="one gain value to a partition"):
-            for t in range(SLOTS):
-                nc.gpsimd.dma_start(gains[t][:], gain_rows[t])
-        bias = keep.tile([P, SLOTS], F32, name="bias")
-        nc.gpsimd.dma_start(bias[:], b2.rearrange("(p j) -> p j", j=SLOTS))
 
         w4_codes = keep.tile([P, PASSES, SLOTS, 2 * P], U8, name="w4_codes", align_bytes=64)
         w4_plane = keep.tile([P, PASSES, SLOTS, P], U8, name="w4_plane", align_bytes=64)
@@ -97,13 +94,21 @@ def tile_list_manifest_paper_scores_kernel(
 
         v_plane = keep.tile([P, PASSES, S], U8, name="v_plane", align_bytes=64)
         nc.vector.memset(v_plane[:].bitcast(I32), 0)
-        picked_bytes = keep.tile([P, S], U8, name="picked_bytes", align_bytes=64)
+        picked_bytes = keep.tile([P, S], U8, name="picked_bytes", tag="picked", align_bytes=64)
         nc.vector.tensor_copy(picked_bytes[:], tab_bytes[:].indirect(idx[:]))
         for quad in range(4):
             nc.scalar.dma_start(
                 v_plane[32 * quad : 32 * quad + 4].bitcast(I32),
                 picked_bytes[8 * quad : 8 * quad + 8, :].bitcast(I32),
             )
+
+        late = keep.tile([P, SLOTS, 8], F32, name="late", tag="picked", align_bytes=64)
+        with nc.allow_non_contiguous_dma(reason="one gain value to a partition"):
+            for t in range(1, SLOTS):
+                nc.sync.dma_start(late[:, t, 0:1], gain_rows[t])
+        gains = [gain0[:]] + [late[:, t, 0:1] for t in range(1, SLOTS)]
+        bias = late[:, 0, 0:SLOTS]
+        nc.sync.dma_start(bias, b2.rearrange("(p j) -> p j", j=SLOTS))
 
         v_codes = [keep.tile([P, S], U32, name="v_codes%d" % a, align_bytes=64) for a in range(PASSES)]
         nc.vector.tensor_copy(v_codes[0][:], table[0][:].bitcast(U32).indirect(idx[:]))
@@ -133,9 +138,9 @@ def tile_list_manifest_paper_scores_kernel(
                     )
                 nc.scalar.activation(squashed[:, lo:hi], acc[:, : hi - lo], ACT.Tanh)
                 if t > 0 or hi <= FIRST_GAIN_SPLIT:
-                    nc.scalar.activation(h[t][:, lo:hi], squashed[:, lo:hi], ACT.Copy, scale=gains[t][:])
+                    nc.scalar.activation(h[t][:, lo:hi], squashed[:, lo:hi], ACT.Copy, scale=gains[t])
                 else:
-                    nc.vector.tensor_scalar(h[t][:, lo:hi], squashed[:, lo:hi], gains[t][:], None, ALU.mult)
+                    nc.vector.tensor_scalar(h[t][:, lo:hi], squashed[:, lo:hi], gains[t], None, ALU.mult)
 
         paper = keep.tile([P, SLOTS, KEPT], F32, name="paper")
         diff = keep.tile([P, SLOTS, KEPT], F32, name="diff")
@@ -146,14 +151,19 @@ def tile_list_manifest_paper_scores_kernel(
                 diff[:, t, lo:hi], a1[t][:].indirect(entries(p3, lo, hi)), paper[:, t, lo:hi], ALU.subtract
             )
 
+        def pick_paper(t, lo, hi):
+            nc.vector.tensor_copy(paper[:, t, lo:hi], h[t][:].indirect(entries(p4, lo, hi)))
+
         for t in range(SLOTS):
             first_stage(t)
             left = ring.tile([P, PAIRS], F32, name="left")
             nc.vector.tensor_copy(left[:], h[t][:].indirect(p1[:]))
-            if t > 0:
-                kept_minus_paper(t - 1, 0, KEPT)
-            nc.vector.tensor_copy(paper[:, t, :], h[t][:].indirect(p4[:]))
+            pick_paper(t, 0, KEPT // 2)
             nc.vector.tensor_tensor(a1[t][:], h[t][:].indirect(p2[:]), left[:], ALU.add)
+            pick_paper(t, KEPT // 2, KEPT)
+            if t < SLOTS - 1:
+                kept_minus_paper(t, 0, KEPT // 2)
+                kept_minus_paper(t, KEPT // 2, KEPT)
 
         w2_grouped = keep.tile([P, SLOTS, P, SLOTS], BF16, name="w2_grouped", align_bytes=64)
         nc.scalar.copy(
@@ -169,22 +179,29 @@ def tile_list_manifest_paper_scores_kernel(
         )
 
         out_rows = out.rearrange("(p j) m -> p j m", j=SLOTS)
-        for c, (lo, hi) in enumerate(TAIL_CHUNKS):
-            width = hi - lo
-            kept_minus_paper(SLOTS - 1, lo, hi)
-            a2 = keep.tile([P, width, SLOTS], BF16, name="a2_%d" % c, align_bytes=64)
+        a2 = [
+            keep.tile([P, hi - lo, SLOTS], BF16, name="a2_%d" % c, align_bytes=64)
+            for c, (lo, hi) in enumerate(TAIL_CHUNKS)
+        ]
+
+        def times_paper(c):
+            lo, hi = TAIL_CHUNKS[c]
             nc.vector.tensor_tensor(
-                a2[:].rearrange("p (c i) t -> p c t i", i=4),
+                a2[c][:].rearrange("p (c i) t -> p c t i", i=4),
                 diff[:, :, lo:hi].rearrange("p t (c i) -> p c t i", i=4),
                 paper[:, :, lo:hi].rearrange("p t (c i) -> p c t i", i=4),
                 ALU.mult,
             )
+
+        def second_stage(c):
+            lo, hi = TAIL_CHUNKS[c]
+            width = hi - lo
             a2_codes = keep.tile([P, width], U32, name="a2_codes%d" % c, align_bytes=64)
             a2_plane = keep.tile([P, width], U8, name="a2_plane%d" % c, align_bytes=64)
             nc.vector.quantize_mx(
                 out=a2_codes[:].bitcast(FP8X4),
                 scales=a2_plane[:],
-                in_=a2[:].rearrange("p m t -> p (m t)"),
+                in_=a2[c][:].rearrange("p m t -> p (m t)"),
             )
             scores = keep.tile([P, SLOTS, width], F32, name="scores%d" % c)
             for j in range(SLOTS):
@@ -200,3 +217,13 @@ def tile_list_manifest_paper_scores_kernel(
                 )
                 nc.scalar.activation(scores[:, j, :], acc[:, :width], ACT.Tanh, bias=bias[:, j : j + 1])
             nc.sync.dma_start(out_rows[:, :, lo:hi], scores[:])
+
+        last = len(TAIL_CHUNKS) - 1
+        kept_minus_paper(SLOTS - 1, *TAIL_CHUNKS[0])
+        for c in range(last + 1):
+            if c < last:
+                kept_minus_paper(SLOTS - 1, *TAIL_CHUNKS[c + 1])
+            times_paper(c)
+            if c > 0:
+                second_stage(c - 1)
+        second_stage(last)

@@ -23,7 +23,7 @@ BANK = 512
 PER_COL = 16
 FIRST_CHUNKS = [(0, 512), (512, 1024), (1024, 1536), (1536, 1792), (1792, 2048)]
 BANK_CHUNKS = [(c, c + BANK) for c in range(0, S, BANK)]
-FIRST_GAIN_SPLIT = 1024
+FIRST_GAIN_SPLIT = 512
 TAIL_CHUNKS = [(0, 256), (256, 384), (384, 512)]
 
 
@@ -46,41 +46,39 @@ def tile_list_manifest_paper_scores_kernel(
         p2 = lists.tile([P, PAIRS // PER_COL], U16, name="p2")
         p3 = lists.tile([P, KEPT // PER_COL], U16, name="p3")
         p4 = lists.tile([P, KEPT // PER_COL], U16, name="p4")
-        nc.sync.dma_start(idx[:], offs)
 
         tab_bytes = keep.tile([P, T], U8, name="tab_bytes", align_bytes=64)
         nc.sync.dma_start(
-            tab_bytes[0:32, :].bitcast(I32),
+            tab_bytes[96:128, :].bitcast(I32),
             tab_scales.rearrange("a q t -> q a t").bitcast(I32),
         )
-        nc.vector.memset(tab_bytes[32:64, :].bitcast(I32), 0)
-        nc.vector.memset(tab_bytes[64:128, :].bitcast(I32), 0)
-
-        w4s_raw = keep.tile([P, PASSES, H // 4], I32, name="w4s_raw", align_bytes=64)
-        w4s_rows = w4_scales.rearrange("a q c -> q a c").bitcast(I32)
-        for quad in range(4):
-            nc.scalar.dma_start(w4s_raw[32 * quad : 32 * quad + 4], w4s_rows[4 * quad : 4 * quad + 4])
-        gain_rows = gain.rearrange("(g t j) -> t g j", t=SLOTS, j=8)
-        gain0 = keep.tile([P, 1], F32, name="gain0")
-        with nc.allow_non_contiguous_dma(reason="one gain value to a partition"):
-            nc.scalar.dma_start(gain0[:], gain_rows[0])
+        nc.sync.dma_start(idx[:], offs)
+        nc.vector.memset(tab_bytes[0:96, :].bitcast(I32), 0)
 
         table = [
             keep.tile([P, T], I32, name="table%d" % a, tag="table%d" % a, align_bytes=64)
             for a in range(PASSES)
         ]
         words = [tab_words[a].rearrange("p n i -> p (n i)").bitcast(I32) for a in range(PASSES)]
-        nc.sync.dma_start(table[0][:], words[0])
-
         w4_raw = keep.tile([P, PASSES, H // 2], I32, name="w4_raw", align_bytes=64)
         nc.sync.dma_start(w4_raw[:], w4_words.rearrange("a p b -> p a b").bitcast(I32))
+        w4s_raw = keep.tile([P, PASSES, H // 4], I32, name="w4s_raw", align_bytes=64)
+        w4s_rows = w4_scales.rearrange("a q c -> q a c").bitcast(I32)
+        for quad in range(4):
+            nc.scalar.dma_start(w4s_raw[32 * quad : 32 * quad + 4], w4s_rows[4 * quad : 4 * quad + 4])
+
+        nc.sync.dma_start(table[0][:], words[0])
+        for half in (slice(0, T // 2), slice(T // 2, T)):
+            nc.sync.dma_start(table[1][:, half], words[1][:, half])
+        gain_rows = gain.rearrange("(g t j) -> t g j", t=SLOTS, j=8)
+        gain0 = keep.tile([P, 1], F32, name="gain0")
+        with nc.allow_non_contiguous_dma(reason="one gain value to a partition"):
+            nc.sync.dma_start(gain0[:], gain_rows[0])
         for tile, src in ((p1, pos1), (p4, pos4), (p2, pos2), (p3, pos3)):
             nc.sync.dma_start(tile[:], src)
-        nc.sync.dma_start(table[1][:], words[1])
 
         w4_codes = keep.tile([P, PASSES, SLOTS, 2 * P], U8, name="w4_codes", align_bytes=64)
         w4_plane = keep.tile([P, PASSES, SLOTS, P], U8, name="w4_plane", align_bytes=64)
-        nc.vector.memset(w4_plane[:].bitcast(I32), 0)
         nc.scalar.copy(
             w4_codes[:].bitcast(U32).rearrange("p a t (g w) -> p a t g w", w=4),
             w4_raw[:].bitcast(U32).rearrange("p a (g t w) -> p a t g w", t=SLOTS, w=4),
@@ -93,13 +91,12 @@ def tile_list_manifest_paper_scores_kernel(
             )
 
         v_plane = keep.tile([P, PASSES, S], U8, name="v_plane", align_bytes=64)
-        nc.vector.memset(v_plane[:].bitcast(I32), 0)
         picked_bytes = keep.tile([P, S], U8, name="picked_bytes", tag="picked", align_bytes=64)
         nc.vector.tensor_copy(picked_bytes[:], tab_bytes[:].indirect(idx[:]))
         for quad in range(4):
             nc.scalar.dma_start(
                 v_plane[32 * quad : 32 * quad + 4].bitcast(I32),
-                picked_bytes[8 * quad : 8 * quad + 8, :].bitcast(I32),
+                picked_bytes[96 + 8 * quad : 96 + 8 * quad + 8, :].bitcast(I32),
             )
 
         late = keep.tile([P, SLOTS, 8], F32, name="late", tag="picked", align_bytes=64)
@@ -111,7 +108,8 @@ def tile_list_manifest_paper_scores_kernel(
         nc.sync.dma_start(bias, b2.rearrange("(p j) -> p j", j=SLOTS))
 
         v_codes = [keep.tile([P, S], U32, name="v_codes%d" % a, align_bytes=64) for a in range(PASSES)]
-        nc.vector.tensor_copy(v_codes[0][:], table[0][:].bitcast(U32).indirect(idx[:]))
+        for lo, hi in ((0, S // 2), (S // 2, S)):
+            nc.vector.tensor_copy(v_codes[0][:, lo:hi], table[0][:].bitcast(U32).indirect(entries(idx, lo, hi)))
         for lo, hi in FIRST_CHUNKS:
             nc.vector.tensor_copy(v_codes[1][:, lo:hi], table[1][:].bitcast(U32).indirect(entries(idx, lo, hi)))
 
@@ -216,7 +214,9 @@ def tile_list_manifest_paper_scores_kernel(
                     stop=True,
                 )
                 nc.scalar.activation(scores[:, j, :], acc[:, :width], ACT.Tanh, bias=bias[:, j : j + 1])
-            nc.sync.dma_start(out_rows[:, :, lo:hi], scores[:])
+                if j % 2 == 1:
+                    queue = nc.sync if j == 1 or c < len(TAIL_CHUNKS) - 1 else nc.scalar
+                    queue.dma_start(out_rows[:, j - 1 : j + 1, lo:hi], scores[:, j - 1 : j + 1, :])
 
         last = len(TAIL_CHUNKS) - 1
         kept_minus_paper(SLOTS - 1, *TAIL_CHUNKS[0])

from contextlib import ExitStack

import concourse.mybir as mybir

K, H, N, T, S, PAIRS, KEPT = 1024, 512, 512, 4096, 2048, 1024, 512
FLOPS = 2 * K * H * S + 2 * H * N * KEPT

F32 = mybir.dt.float32
BF16 = mybir.dt.bfloat16
I32 = mybir.dt.int32
U32 = mybir.dt.uint32
U16 = mybir.dt.uint16
U8 = mybir.dt.uint8
FP8X4 = mybir.dt.float8_e4m3fn_x4
FP4X4 = mybir.dt.float4_e2m1fn_x4
ACT = mybir.ActivationFunctionType
ALU = mybir.AluOpType

P = 128
PASSES = 2
SLOTS = 4
BANK = 512
PER_COL = 16
FIRST_CHUNKS = [(0, 512), (512, 1024), (1024, 1536), (1536, 1792), (1792, 2048)]
BANK_CHUNKS = [(c, c + BANK) for c in range(0, S, BANK)]
FIRST_GAIN_SPLIT = 512
TAIL_CHUNKS = [(0, 256), (256, 384), (384, 512)]


def entries(lst, lo, hi):
    return lst[:, lo // PER_COL : hi // PER_COL]


def tile_list_manifest_paper_scores_kernel(
    tc, tab_words, tab_scales, w4_words, w4_scales, gain, w2, b2, offs, pos1, pos2, pos3, pos4, out
):
    nc = tc.nc
    with ExitStack() as ctx:
        lists = ctx.enter_context(tc.tile_pool(name="lists", bufs=1))
        keep = ctx.enter_context(tc.tile_pool(name="keep", bufs=1))
        ring = ctx.enter_context(tc.tile_pool(name="ring", bufs=2))
        psum = ctx.enter_context(tc.psum_pool(name="psum", bufs=8))

        idx = lists.tile([P, S // PER_COL], U16, name="idx")
        p1 = lists.tile([P, PAIRS // PER_COL], U16, name="p1")
        p2 = lists.tile([P, PAIRS // PER_COL], U16, name="p2")
        p3 = lists.tile([P, KEPT // PER_COL], U16, name="p3")
        p4 = lists.tile([P, KEPT // PER_COL], U16, name="p4")

        tab_bytes = keep.tile([P, T], U8, name="tab_bytes", align_bytes=64)
        nc.sync.dma_start(
            tab_bytes[96:128, :].bitcast(I32),
            tab_scales.rearrange("a q t -> q a t").bitcast(I32),
        )
        nc.sync.dma_start(idx[:], offs)
        nc.vector.memset(tab_bytes[0:96, :].bitcast(I32), 0)

        table = [
            keep.tile([P, T], I32, name="table%d" % a, tag="table%d" % a, align_bytes=64)
            for a in range(PASSES)
        ]
        words = [tab_words[a].rearrange("p n i -> p (n i)").bitcast(I32) for a in range(PASSES)]
        w4_raw = keep.tile([P, PASSES, H // 2], I32, name="w4_raw", align_bytes=64)
        nc.sync.dma_start(w4_raw[:], w4_words.rearrange("a p b -> p a b").bitcast(I32))
        w4s_raw = keep.tile([P, PASSES, H // 4], I32, name="w4s_raw", align_bytes=64)
        w4s_rows = w4_scales.rearrange("a q c -> q a c").bitcast(I32)
        for quad in range(4):
            nc.scalar.dma_start(w4s_raw[32 * quad : 32 * quad + 4], w4s_rows[4 * quad : 4 * quad + 4])

        nc.sync.dma_start(table[0][:], words[0])
        for half in (slice(0, T // 2), slice(T // 2, T)):
            nc.sync.dma_start(table[1][:, half], words[1][:, half])
        gain_rows = gain.rearrange("(g t j) -> t g j", t=SLOTS, j=8)
        gain0 = keep.tile([P, 1], F32, name="gain0")
        with nc.allow_non_contiguous_dma(reason="one gain value to a partition"):
            nc.sync.dma_start(gain0[:], gain_rows[0])
        for tile, src in ((p1, pos1), (p4, pos4), (p2, pos2), (p3, pos3)):
            nc.sync.dma_start(tile[:], src)

        w4_codes = keep.tile([P, PASSES, SLOTS, 2 * P], U8, name="w4_codes", align_bytes=64)
        w4_plane = keep.tile([P, PASSES, SLOTS, P], U8, name="w4_plane", align_bytes=64)
        nc.scalar.copy(
            w4_codes[:].bitcast(U32).rearrange("p a t (g w) -> p a t g w", w=4),
            w4_raw[:].bitcast(U32).rearrange("p a (g t w) -> p a t g w", t=SLOTS, w=4),
        )
        for quad in range(4):
            rows = slice(32 * quad, 32 * quad + 4)
            nc.scalar.copy(
                w4_plane[rows].bitcast(U32).rearrange("p a t (g w) -> p a t g w", w=2),
                w4s_raw[rows].bitcast(U32).rearrange("p a (g t w) -> p a t g w", t=SLOTS, w=2),
            )

        v_plane = keep.tile([P, PASSES, S], U8, name="v_plane", align_bytes=64)
        picked_bytes = keep.tile([P, S], U8, name="picked_bytes", tag="picked", align_bytes=64)
        nc.vector.tensor_copy(picked_bytes[:], tab_bytes[:].indirect(idx[:]))
        for quad in range(4):
            nc.scalar.dma_start(
                v_plane[32 * quad : 32 * quad + 4].bitcast(I32),
                picked_bytes[96 + 8 * quad : 96 + 8 * quad + 8, :].bitcast(I32),
            )

        late = keep.tile([P, SLOTS, 8], F32, name="late", tag="picked", align_bytes=64)
        with nc.allow_non_contiguous_dma(reason="one gain value to a partition"):
            for t in range(1, SLOTS):
                nc.sync.dma_start(late[:, t, 0:1], gain_rows[t])
        gains = [gain0[:]] + [late[:, t, 0:1] for t in range(1, SLOTS)]
        bias = late[:, 0, 0:SLOTS]
        nc.sync.dma_start(bias, b2.rearrange("(p j) -> p j", j=SLOTS))

        v_codes = [keep.tile([P, S], U32, name="v_codes%d" % a, align_bytes=64) for a in range(PASSES)]
        for lo, hi in ((0, S // 2), (S // 2, S)):
            nc.vector.tensor_copy(v_codes[0][:, lo:hi], table[0][:].bitcast(U32).indirect(entries(idx, lo, hi)))
        for lo, hi in FIRST_CHUNKS:
            nc.vector.tensor_copy(v_codes[1][:, lo:hi], table[1][:].bitcast(U32).indirect(entries(idx, lo, hi)))

        w2_raw = keep.tile([P, SLOTS, N], F32, name="w2_raw", tag="table0", align_bytes=64)
        w2_rows = w2.rearrange("(g t j) n -> t g j n", t=SLOTS, j=8)
        for t in range(SLOTS):
            nc.sync.dma_start(w2_raw[:, t, :], w2_rows[t])

        h = [keep.tile([P, S], F32, name="h%d" % t) for t in range(SLOTS)]

        def first_stage(t):
            squashed = ring.tile([P, S], F32, name="squashed")
            for lo, hi in FIRST_CHUNKS if t == 0 else BANK_CHUNKS:
                acc = psum.tile([P, BANK], F32, name="acc")
                for a in range(PASSES):
                    nc.tensor.matmul_mx(
                        out=acc[:, : hi - lo],
                        lhsT=w4_codes[:, a, t, :].bitcast(FP4X4),
                        lhsT_scale=w4_plane[:, a, t, :],
                        rhs=v_codes[a][:, lo:hi].bitcast(FP8X4),
                        rhs_scale=v_plane[:, a, lo:hi],
                        start=(a == 0),
                        stop=(a == PASSES - 1),
                    )
                nc.scalar.activation(squashed[:, lo:hi], acc[:, : hi - lo], ACT.Tanh)
                if t > 0 or hi <= FIRST_GAIN_SPLIT:
                    nc.scalar.activation(h[t][:, lo:hi], squashed[:, lo:hi], ACT.Copy, scale=gains[t])
                else:
                    nc.vector.tensor_scalar(h[t][:, lo:hi], squashed[:, lo:hi], gains[t], None, ALU.mult)

        paper = keep.tile([P, SLOTS, KEPT], F32, name="paper")
        diff = keep.tile([P, SLOTS, KEPT], F32, name="diff")
        a1 = [keep.tile([P, PAIRS], F32, name="a1_%d" % t) for t in range(SLOTS)]

        def kept_minus_paper(t, lo, hi):
            nc.vector.tensor_tensor(
                diff[:, t, lo:hi], a1[t][:].indirect(entries(p3, lo, hi)), paper[:, t, lo:hi], ALU.subtract
            )

        def pick_paper(t, lo, hi):
            nc.vector.tensor_copy(paper[:, t, lo:hi], h[t][:].indirect(entries(p4, lo, hi)))

        for t in range(SLOTS):
            first_stage(t)
            left = ring.tile([P, PAIRS], F32, name="left")
            nc.vector.tensor_copy(left[:], h[t][:].indirect(p1[:]))
            pick_paper(t, 0, KEPT // 2)
            nc.vector.tensor_tensor(a1[t][:], h[t][:].indirect(p2[:]), left[:], ALU.add)
            pick_paper(t, KEPT // 2, KEPT)
            if t < SLOTS - 1:
                kept_minus_paper(t, 0, KEPT // 2)
                kept_minus_paper(t, KEPT // 2, KEPT)

        w2_grouped = keep.tile([P, SLOTS, P, SLOTS], BF16, name="w2_grouped", align_bytes=64)
        nc.scalar.copy(
            w2_grouped[:].rearrange("p j m t -> p m t j"),
            w2_raw[:].rearrange("p t (m j) -> p m t j", j=SLOTS),
        )
        w2_codes = keep.tile([P, N], U32, name="w2_codes", align_bytes=64)
        w2_plane = keep.tile([P, N], U8, name="w2_plane", align_bytes=64)
        nc.vector.quantize_mx(
            out=w2_codes[:].bitcast(FP8X4),
            scales=w2_plane[:],
            in_=w2_grouped[:].rearrange("p j m t -> p (j m t)"),
        )

        out_rows = out.rearrange("(p j) m -> p j m", j=SLOTS)
        a2 = [
            keep.tile([P, hi - lo, SLOTS], BF16, name="a2_%d" % c, align_bytes=64)
            for c, (lo, hi) in enumerate(TAIL_CHUNKS)
        ]

        def times_paper(c):
            lo, hi = TAIL_CHUNKS[c]
            nc.vector.tensor_tensor(
                a2[c][:].rearrange("p (c i) t -> p c t i", i=4),
                diff[:, :, lo:hi].rearrange("p t (c i) -> p c t i", i=4),
                paper[:, :, lo:hi].rearrange("p t (c i) -> p c t i", i=4),
                ALU.mult,
            )

        def second_stage(c):
            lo, hi = TAIL_CHUNKS[c]
            width = hi - lo
            a2_codes = keep.tile([P, width], U32, name="a2_codes%d" % c, align_bytes=64)
            a2_plane = keep.tile([P, width], U8, name="a2_plane%d" % c, align_bytes=64)
            nc.vector.quantize_mx(
                out=a2_codes[:].bitcast(FP8X4),
                scales=a2_plane[:],
                in_=a2[c][:].rearrange("p m t -> p (m t)"),
            )
            scores = keep.tile([P, SLOTS, width], F32, name="scores%d" % c)
            for j in range(SLOTS):
                acc = psum.tile([P, BANK], F32, name="acc")
                nc.tensor.matmul_mx(
                    out=acc[:, :width],
                    lhsT=w2_codes[:, j * P : (j + 1) * P].bitcast(FP8X4),
                    lhsT_scale=w2_plane[:, j * P : (j + 1) * P],
                    rhs=a2_codes[:].bitcast(FP8X4),
                    rhs_scale=a2_plane[:],
                    start=True,
                    stop=True,
                )
                nc.scalar.activation(scores[:, j, :], acc[:, :width], ACT.Tanh, bias=bias[:, j : j + 1])
                if j % 2 == 1:
                    queue = nc.sync if j == 1 or c < len(TAIL_CHUNKS) - 1 else nc.scalar
                    queue.dma_start(out_rows[:, j - 1 : j + 1, lo:hi], scores[:, j - 1 : j + 1, :])

        last = len(TAIL_CHUNKS) - 1
        kept_minus_paper(SLOTS - 1, *TAIL_CHUNKS[0])
        for c in range(last + 1):
            if c < last:
                kept_minus_paper(SLOTS - 1, *TAIL_CHUNKS[c + 1])
            times_paper(c)
            if c > 0:
                second_stage(c - 1)
        second_stage(last)
